import numpy as np
import ml_dtypes


def mxq(x, axis, fmt="e4m3"):
    dtype, down = {"e4m3": (ml_dtypes.float8_e4m3fn, 7), "e5m2": (ml_dtypes.float8_e5m2, 14)}[fmt]
    v = np.moveaxis(np.asarray(x, np.float32).astype(ml_dtypes.bfloat16).astype(np.float64), axis, -1)
    blocks = v.reshape(v.shape[:-1] + (-1, 32))
    amax = np.abs(blocks).max(-1, keepdims=True)
    byte = np.maximum(np.where(amax > 0, np.frexp(amax)[1] - 1 + 127, 0) - down, 1)
    scale = np.exp2(byte - 127.0)
    codes = (blocks / scale).astype(np.float32).astype(dtype).astype(np.float64)
    return np.moveaxis((codes * scale).reshape(v.shape), -1, axis)


WIDE = False


def mx_kscale(k):
    if not WIDE:
        return np.ones(k)
    levels = np.array([10, -10, 5, -5, 0])
    if k % 512:
        return np.exp2(np.random.permutation(np.resize(levels, k // 32))).repeat(32)
    a = np.empty((k // 512, 16))
    for p in range(k // 512):
        a[p, :8] = np.random.permutation(np.resize(levels, 8))
        for g in range(8):
            far = levels[np.abs(levels - a[p, g]) >= 10]
            a[p, g + 8] = far[np.random.randint(len(far))]
    return np.exp2(a.ravel()).repeat(32)


def f64(x):
    return np.asarray(x).astype(np.float64)


def striped(idx):
    return np.tile(idx.reshape(-1, 16).T, (8, 1)).astype(np.uint16)


def unstriped(offs):
    return offs[:16].T.reshape(-1).astype(np.int64)


def pack_weight(w):
    k, n = w.shape
    w = f64(np.asarray(w, np.float32).astype(ml_dtypes.bfloat16)).reshape(k // 32, 32, n)
    amax = np.abs(w).max(1)
    byte = np.clip(np.where(amax > 0, np.frexp(amax)[1] - 1 + 127 - 7, 1), 1, 254)
    scaled = (w * np.exp2(127.0 - byte)[:, None, :]).reshape(k, n).astype(np.float32)
    words = np.ascontiguousarray(scaled.reshape(k // 512, 128, 4, n).transpose(0, 1, 3, 2)).astype(ml_dtypes.float8_e4m3fn).view(np.uint8)
    return words, np.ascontiguousarray(byte.astype(np.uint8).reshape(k // 512, 16, n))


def unpack_weight(words, scales):
    g, p, n, _ = words.shape
    vals = np.ascontiguousarray(words).view(ml_dtypes.float8_e4m3fn).astype(np.float64) * np.repeat(np.exp2(scales.astype(np.float64) - 127.0), 8, axis=1)[..., None]
    return vals.transpose(0, 1, 3, 2).reshape(g * 512, n)


def relu(v):
    return np.maximum(v, 0.0)

def planes(y):
    n, m = y.shape
    v = y.astype(np.float32).astype(ml_dtypes.bfloat16).astype(np.float64).reshape(n // 32, 32, m)
    top = np.abs(v).max(1)
    byte = np.clip(np.where(top > 0, np.frexp(top)[1] - 1 + 127 - 7, 1), 1, 254)
    codes = (v * np.exp2(127.0 - byte)[:, None, :]).reshape(n, m).astype(np.float32).astype(ml_dtypes.float8_e4m3fn).view(np.uint8)
    words = codes.reshape(n // 512, 128, 4, m).transpose(0, 1, 3, 2)
    return np.ascontiguousarray(words), np.ascontiguousarray(byte.astype(np.uint8).reshape(n // 512, 16, m))


K, T, S, V, H, J = 512, 2048, 1024, 512, 512, 512


def setup_inputs():
    n = np.random.standard_normal
    s = mx_kscale(K)[:, None]
    u = mx_kscale(H)
    r = mx_kscale(J)[:, None]
    packed_xT = pack_weight(n((K, T)) * s)
    return {
        "x_words": packed_xT[0],
        "x_scales": packed_xT[1],
        "eT": (n((J, V)) * r).astype(np.float32),
        "w1": (n((K, H)) / np.sqrt(3 * K) / s * u).astype(np.float32),
        "w2": (n((K, H)) / np.sqrt(3 * K) / s * u).astype(np.float32),
        "w3": (n((J, H)) / np.sqrt(3 * J) / r * u).astype(np.float32),
        "w4": (n((H, H)) / np.sqrt(H) / u[:, None]).astype(np.float32),
        "offs": striped(np.random.permutation(T)[:S]),
    }


def reference(x_words, x_scales, eT, w1, w2, w3, w4, offs):
    xq = unpack_weight(x_words, x_scales)[:, unstriped(offs)]
    h = relu(mxq(f64(w1), 0, "e4m3").T @ xq[:, :V] + mxq(f64(w2), 0, "e4m3").T @ xq[:, V:2 * V] + mxq(f64(w3), 0, "e4m3").T @ mxq(f64(eT), 0, "e4m3"))
    out_0 = mxq(f64(w4), 0, "e4m3").T @ mxq(h, 0, "e4m3")
    return (out_0,) + planes(out_0)

@@ -1,0 +1,181 @@
+from contextlib import ExitStack
+
+import concourse.mybir as mybir
+
+K, T, S, V, H = 512, 2048, 1024, 512, 512
+FLOPS = 4 * 2 * 512 * 512 * 512
+
+F32 = mybir.dt.float32
+BF16 = mybir.dt.bfloat16
+U32 = mybir.dt.uint32
+I32 = mybir.dt.int32
+U16 = mybir.dt.uint16
+U8 = mybir.dt.uint8
+FP8X4 = mybir.dt.float8_e4m3fn_x4
+COPY = mybir.ActivationFunctionType.Copy
+RELU = mybir.ActivationFunctionType.Relu
+
+P = 128
+PACK = 4
+CHUNK = 128
+N_CHUNKS = V // CHUNK
+HALF = V // 2
+
+
+def quantize(nc, codes, scales, values):
+    nc.vector.quantize_mx(out=codes.bitcast(FP8X4), scales=scales, in_=values)
+
+
+def tile_picked_edgeup_relu_po_kernel(
+    tc, x_words, x_scales, eT, w1, w2, w3, w4, offs, out_0, out_1, out_2
+):
+    nc = tc.nc
+    with ExitStack() as ctx:
+        keep = ctx.enter_context(tc.tile_pool(name="keep", bufs=1))
+        psum = ctx.enter_context(tc.psum_pool(name="psum", bufs=1))
+
+        def sb(name, shape, dtype):
+            return keep.tile(shape, dtype, name=name, align_bytes=64)
+
+        offsets = keep.tile([P, S // 16], U16, name="offsets")
+        node_words = sb("node_words", [P, T], U32)
+        node_scales = sb("node_scales", [P, T], U8)
+
+        nc.vector.memset(node_scales[:].bitcast(I32), 0)
+        nc.sync.dma_start(offsets[:], offs)
+        words_dram = x_words[0].rearrange("p n t -> p (n t)").bitcast(I32)
+        nc.sync.dma_start(node_words[:, : T // 4].bitcast(I32), words_dram[:, : T // 4])
+        for q in range(4):
+            nc.sync.dma_start(
+                node_scales[32 * q : 32 * q + 4, :].bitcast(I32),
+                x_scales[0][4 * q : 4 * q + 4, :].bitcast(I32),
+            )
+        nc.sync.dma_start(node_words[:, T // 4 :].bitcast(I32), words_dram[:, T // 4 :])
+
+        def load_rows(name, src):
+            raw = sb(name, [P, PACK, src.shape[1]], F32)
+            nc.sync.dma_start(raw[:], src.rearrange("(p j) c -> p j c", j=PACK))
+            return raw
+
+        w_raw = [load_rows("w1_raw", w1), load_rows("w2_raw", w2), load_rows("w3_raw", w3)]
+        e_raw = [load_rows("e_raw%d" % a, eT[:, a * HALF : (a + 1) * HALF]) for a in range(2)]
+        w_raw.append(load_rows("w4_raw", w4))
+
+        end_scales = sb("end_scales", [P, S], U8)
+        end_words = sb("end_words", [P, S], U32)
+        nc.vector.tensor_copy(end_scales[:], node_scales[:].indirect(offsets[:]))
+        nc.vector.tensor_copy(end_words[:], node_words[:].indirect(offsets[:]))
+
+        def quantize_weight(i):
+            src = w_raw[i][:].rearrange("p j (m t) -> p m j t", t=PACK)
+            parts = {}
+            for u in (1, 0):
+                grouped = sb("w%d_grouped%d" % (i, u), [P, 2 * P * PACK], BF16)
+                dst = grouped[:].rearrange("p (t m j) -> p m j t", t=2, j=PACK)
+                if u == 0 or i == 0:
+                    nc.scalar.activation(dst, src[:, :, :, 2 * u : 2 * u + 2], COPY)
+                else:
+                    nc.vector.tensor_copy(dst, src[:, :, :, 2:4])
+                codes = sb("w%d_codes%d" % (i, u), [P, 2 * P], U32)
+                scales = sb("w%d_scales%d" % (i, u), [P, 2 * P], U8)
+                quantize(nc, codes[:], scales[:], grouped[:])
+                for s in range(2):
+                    parts[2 * u + s] = (codes[:, s * P : (s + 1) * P], scales[:, s * P : (s + 1) * P])
+            return parts
+
+        h_banks = [psum.tile([P, PACK, CHUNK], F32, name="h_bank%d" % c) for c in range(N_CHUNKS)]
+        T_ORDER = (2, 3, 0, 1)
+
+        def h_pass(c, t, weight, codes, scales, start, stop):
+            nc.tensor.matmul_mx(
+                out=h_banks[c][:, t, :],
+                lhsT=weight[t][0].bitcast(FP8X4),
+                lhsT_scale=weight[t][1],
+                rhs=codes.bitcast(FP8X4),
+                rhs_scale=scales,
+                start=start,
+                stop=stop,
+            )
+
+        for side in range(2):
+            weight = quantize_weight(side)
+            for t in T_ORDER:
+                for c in range(N_CHUNKS):
+                    cols = slice(side * V + c * CHUNK, side * V + (c + 1) * CHUNK)
+                    h_pass(c, t, weight, end_words[:, cols], end_scales[:, cols], side == 0 and t == T_ORDER[0], False)
+        w3_q = quantize_weight(2)
+
+        h_codes = sb("h_codes", [P, V], U32)
+        h_scales = sb("h_scales", [P, V], U8)
+
+        def edge_chunk(c):
+            raw = e_raw[c // 2][:, :, (c % 2) * CHUNK : (c % 2 + 1) * CHUNK]
+            grouped = sb("e_grouped%d" % c, [P, CHUNK * PACK], BF16)
+            src = raw.rearrange("p j (g i) -> p g j i", i=4)
+            dst = grouped[:].rearrange("p (g i j) -> p g j i", i=4, j=PACK)
+            if c % 2 == 0:
+                nc.vector.tensor_copy(dst, src)
+            else:
+                nc.scalar.activation(dst, src, COPY)
+            codes = sb("e_codes%d" % c, [P, CHUNK], U32)
+            scales = sb("e_scales%d" % c, [P, CHUNK], U8)
+            quantize(nc, codes[:], scales[:], grouped[:])
+            for t in T_ORDER:
+                h_pass(c, t, w3_q, codes[:], scales[:], False, t == T_ORDER[-1])
+
+        def hidden_chunk(c):
+            grouped = sb("h_grouped%d" % c, [P, CHUNK * PACK], BF16)
+            dst = grouped[:].rearrange("p (v t) -> p v t", t=PACK)
+            src = h_banks[c][:].rearrange("p t v -> p v t")
+            if c == 2:
+                nc.vector.tensor_scalar_max(dst, src, 0.0)
+            else:
+                nc.scalar.activation(dst, src, RELU)
+            cols = slice(c * CHUNK, (c + 1) * CHUNK)
+            quantize(nc, h_codes[:, cols], h_scales[:, cols], grouped[:])
+
+        for c in range(N_CHUNKS):
+            edge_chunk(c)
+        for c in range(N_CHUNKS):
+            hidden_chunk(c)
+
+        w4_q = quantize_weight(3)
+        result = sb("result", [P, PACK, V], F32)
+        out_rows = out_0.rearrange("(p t) v -> p t v", t=PACK)
+        for n, t in enumerate(T_ORDER):
+            bank = psum.tile([P, V], F32, name="out_bank%d" % t)
+            nc.tensor.matmul_mx(
+                out=bank[:],
+                lhsT=w4_q[t][0].bitcast(FP8X4),
+                lhsT_scale=w4_q[t][1],
+                rhs=h_codes[:].bitcast(FP8X4),
+                rhs_scale=h_scales[:],
+                start=True,
+                stop=True,
+            )
+            if n % 2 == 0:
+                nc.scalar.activation(result[:, t, :], bank[:], COPY)
+            else:
+                nc.vector.tensor_copy(result[:, t, :], bank[:])
+            nc.sync.dma_start(out_rows[:, t, :], result[:, t, :])
+
+        y_codes = sb("y_codes", [P, V], U32)
+        y_scales = sb("y_scales", [P, V], U8)
+        codes_dram = out_1[0].rearrange("p n t -> p (n t)").bitcast(I32)
+        for a in range(2):
+            cols = slice(a * HALF, (a + 1) * HALF)
+            grouped = sb("y_grouped%d" % a, [P, HALF * PACK], BF16)
+            src = result[:, :, cols].rearrange("p t (g i) -> p g t i", i=4)
+            dst = grouped[:].rearrange("p (g i t) -> p g t i", i=4, t=PACK)
+            if a == 0:
+                nc.vector.tensor_copy(dst, src)
+            else:
+                nc.scalar.activation(dst, src, COPY)
+            quantize(nc, y_codes[:, cols], y_scales[:, cols], grouped[:])
+            nc.sync.dma_start(codes_dram[:, cols], y_codes[:, cols].bitcast(I32))
+        for q in range(4):
+            queue = nc.sync if q % 2 == 0 else nc.scalar
+            queue.dma_start(
+                out_2[0][4 * q : 4 * q + 4, :].bitcast(I32),
+                y_scales[32 * q : 32 * q + 4, :].bitcast(I32),
+            )

@@ -42,24 +42,29 @@ def tile_picked_edgeup_relu_po_kernel(
         node_scales = sb("node_scales", [P, T], U8)
 
         nc.vector.memset(node_scales[:].bitcast(I32), 0)
-        nc.sync.dma_start(offsets[:], offs)
-        words_dram = x_words[0].rearrange("p n t -> p (n t)").bitcast(I32)
-        nc.sync.dma_start(node_words[:, : T // 4].bitcast(I32), words_dram[:, : T // 4])
-        for q in range(4):
-            nc.sync.dma_start(
-                node_scales[32 * q : 32 * q + 4, :].bitcast(I32),
-                x_scales[0][4 * q : 4 * q + 4, :].bitcast(I32),
-            )
-        nc.sync.dma_start(node_words[:, T // 4 :].bitcast(I32), words_dram[:, T // 4 :])
 
         def load_rows(name, src):
             raw = sb(name, [P, PACK, src.shape[1]], F32)
             nc.sync.dma_start(raw[:], src.rearrange("(p j) c -> p j c", j=PACK))
             return raw
 
-        w_raw = [load_rows("w1_raw", w1), load_rows("w2_raw", w2), load_rows("w3_raw", w3)]
-        e_raw = [load_rows("e_raw%d" % a, eT[:, a * HALF : (a + 1) * HALF]) for a in range(2)]
-        w_raw.append(load_rows("w4_raw", w4))
+        def load_halves(name, src):
+            return [load_rows("%s%d" % (name, a), src[:, a * HALF : (a + 1) * HALF]) for a in range(2)]
+
+        w1_raw = [load_rows("w1_raw0", w1[:, :HALF])]
+        nc.sync.dma_start(offsets[:], offs)
+        for q in range(4):
+            nc.sync.dma_start(
+                node_scales[32 * q : 32 * q + 4, :].bitcast(I32),
+                x_scales[0][4 * q : 4 * q + 4, :].bitcast(I32),
+            )
+        w1_raw.append(load_rows("w1_raw1", w1[:, HALF:]))
+        nc.sync.dma_start(node_words[:].bitcast(I32), x_words[0].rearrange("p n t -> p (n t)").bitcast(I32))
+        w3_raw = [load_rows("w3_raw", w3)]
+        w_raw = [w1_raw, load_halves("w2_raw", w2), w3_raw]
+        e_raw = load_halves("e_raw", eT)
+        w_raw.append(load_halves("w4_raw", w4))
+        ON_VECTOR = {(2, 0, 1), (1, 1, 1), (3, 0, 0), (3, 0, 1), (3, 1, 1)}
 
         end_scales = sb("end_scales", [P, S], U8)
         end_words = sb("end_words", [P, S], U32)
@@ -67,18 +72,23 @@ def tile_picked_edgeup_relu_po_kernel(
         nc.vector.tensor_copy(end_words[:], node_words[:].indirect(offsets[:]))
 
         def quantize_weight(i):
-            src = w_raw[i][:].rearrange("p j (m t) -> p m j t", t=PACK)
+            grouped = [sb("w%d_grouped%d" % (i, u), [P, 2 * P * PACK], BF16) for u in range(2)]
+            m0 = 0
+            for n, raw in enumerate(w_raw[i]):
+                src = raw[:].rearrange("p j (m t) -> p m j t", t=PACK)
+                m1 = m0 + src.shape[1]
+                for u in (1, 0):
+                    dst = grouped[u][:].rearrange("p (t m j) -> p m j t", t=2, j=PACK)[:, m0:m1, :, :]
+                    if (i, n, u) not in ON_VECTOR:
+                        nc.scalar.activation(dst, src[:, :, :, 2 * u : 2 * u + 2], COPY)
+                    else:
+                        nc.vector.tensor_copy(dst, src[:, :, :, 2 * u : 2 * u + 2])
+                m0 = m1
             parts = {}
             for u in (1, 0):
-                grouped = sb("w%d_grouped%d" % (i, u), [P, 2 * P * PACK], BF16)
-                dst = grouped[:].rearrange("p (t m j) -> p m j t", t=2, j=PACK)
-                if u == 0 or i == 0:
-                    nc.scalar.activation(dst, src[:, :, :, 2 * u : 2 * u + 2], COPY)
-                else:
-                    nc.vector.tensor_copy(dst, src[:, :, :, 2:4])
                 codes = sb("w%d_codes%d" % (i, u), [P, 2 * P], U32)
                 scales = sb("w%d_scales%d" % (i, u), [P, 2 * P], U8)
-                quantize(nc, codes[:], scales[:], grouped[:])
+                quantize(nc, codes[:], scales[:], grouped[u][:])
                 for s in range(2):
                     parts[2 * u + s] = (codes[:, s * P : (s + 1) * P], scales[:, s * P : (s + 1) * P])
             return parts
@@ -97,81 +107,109 @@ def tile_picked_edgeup_relu_po_kernel(
                 stop=stop,
             )
 
-        for side in range(2):
-            weight = quantize_weight(side)
+        def node_passes(side, weight, c):
+            cols = slice(side * V + c * CHUNK, side * V + (c + 1) * CHUNK)
             for t in T_ORDER:
-                for c in range(N_CHUNKS):
-                    cols = slice(side * V + c * CHUNK, side * V + (c + 1) * CHUNK)
-                    h_pass(c, t, weight, end_words[:, cols], end_scales[:, cols], side == 0 and t == T_ORDER[0], False)
+                h_pass(c, t, weight, end_words[:, cols], end_scales[:, cols], side == 0 and t == T_ORDER[0], False)
+
+        w1_q = quantize_weight(0)
+        for c in range(N_CHUNKS):
+            node_passes(0, w1_q, c)
         w3_q = quantize_weight(2)
+        w2_q = quantize_weight(1)
 
         h_codes = sb("h_codes", [P, V], U32)
         h_scales = sb("h_scales", [P, V], U8)
 
-        def edge_chunk(c):
-            raw = e_raw[c // 2][:, :, (c % 2) * CHUNK : (c % 2 + 1) * CHUNK]
-            grouped = sb("e_grouped%d" % c, [P, CHUNK * PACK], BF16)
-            src = raw.rearrange("p j (g i) -> p g j i", i=4)
+        def edge_half(a):
+            grouped = sb("e_grouped%d" % a, [P, HALF * PACK], BF16)
+            src = e_raw[a][:].rearrange("p j (g i) -> p g j i", i=4)
             dst = grouped[:].rearrange("p (g i j) -> p g j i", i=4, j=PACK)
-            if c % 2 == 0:
-                nc.vector.tensor_copy(dst, src)
-            else:
-                nc.scalar.activation(dst, src, COPY)
-            codes = sb("e_codes%d" % c, [P, CHUNK], U32)
-            scales = sb("e_scales%d" % c, [P, CHUNK], U8)
+            nc.vector.tensor_copy(dst[:, :32], src[:, :32])
+            nc.scalar.activation(dst[:, 32:], src[:, 32:], COPY)
+            codes = sb("e_codes%d" % a, [P, HALF], U32)
+            scales = sb("e_scales%d" % a, [P, HALF], U8)
             quantize(nc, codes[:], scales[:], grouped[:])
-            for t in T_ORDER:
-                h_pass(c, t, w3_q, codes[:], scales[:], False, t == T_ORDER[-1])
+            for s in range(2):
+                c = 2 * a + s
+                cols = slice(s * CHUNK, (s + 1) * CHUNK)
+                for t in T_ORDER:
+                    h_pass(c, t, w3_q, codes[:, cols], scales[:, cols], False, t == T_ORDER[-1])
 
-        def hidden_chunk(c):
-            grouped = sb("h_grouped%d" % c, [P, CHUNK * PACK], BF16)
-            dst = grouped[:].rearrange("p (v t) -> p v t", t=PACK)
-            src = h_banks[c][:].rearrange("p t v -> p v t")
-            if c == 2:
-                nc.vector.tensor_scalar_max(dst, src, 0.0)
-            else:
-                nc.scalar.activation(dst, src, RELU)
-            cols = slice(c * CHUNK, (c + 1) * CHUNK)
+        out_banks = [psum.tile([P, 2, HALF], F32, name="out_bank%d" % n) for n in range(4)]
+
+        def warm(first, count):
+            cols = slice(first, first + HALF)
+            for n in range(count):
+                nc.tensor.matmul_mx(
+                    out=out_banks[n][:, 0, :],
+                    lhsT=w3_q[n][0].bitcast(FP8X4),
+                    lhsT_scale=w3_q[n][1],
+                    rhs=h_codes[:, cols].bitcast(FP8X4),
+                    rhs_scale=h_scales[:, cols],
+                    start=True,
+                    stop=True,
+                )
+
+        def hidden_half(a):
+            grouped = sb("h_grouped%d" % a, [P, HALF * PACK], BF16)
+            for s in range(2):
+                dst = grouped[:, s * CHUNK * PACK : (s + 1) * CHUNK * PACK].rearrange("p (v t) -> p v t", t=PACK)
+                nc.scalar.activation(dst, h_banks[2 * a + s][:].rearrange("p t v -> p v t"), RELU)
+            cols = slice(a * HALF, (a + 1) * HALF)
             quantize(nc, h_codes[:, cols], h_scales[:, cols], grouped[:])
 
-        for c in range(N_CHUNKS):
-            edge_chunk(c)
-        for c in range(N_CHUNKS):
-            hidden_chunk(c)
-
+        for a in range(2):
+            node_passes(1, w2_q, 2 * a)
+            node_passes(1, w2_q, 2 * a + 1)
+            edge_half(a)
+        hidden_half(0)
+        warm(0, 4)
         w4_q = quantize_weight(3)
-        result = sb("result", [P, PACK, V], F32)
+        hidden_half(1)
+
         out_rows = out_0.rearrange("(p t) v -> p t v", t=PACK)
-        for n, t in enumerate(T_ORDER):
-            bank = psum.tile([P, V], F32, name="out_bank%d" % t)
-            nc.tensor.matmul_mx(
-                out=bank[:],
-                lhsT=w4_q[t][0].bitcast(FP8X4),
-                lhsT_scale=w4_q[t][1],
-                rhs=h_codes[:].bitcast(FP8X4),
-                rhs_scale=h_scales[:],
-                start=True,
-                stop=True,
-            )
-            if n % 2 == 0:
-                nc.scalar.activation(result[:, t, :], bank[:], COPY)
-            else:
-                nc.vector.tensor_copy(result[:, t, :], bank[:])
-            nc.sync.dma_start(out_rows[:, t, :], result[:, t, :])
+        results = [sb("result%d" % a, [P, PACK, HALF], F32) for a in range(2)]
+        for a in range(2):
+            cols = slice(a * HALF, (a + 1) * HALF)
+            for u in (1, 0):
+                bank = out_banks[2 * a + u]
+                for s in range(2):
+                    t = 2 * u + s
+                    nc.tensor.matmul_mx(
+                        out=bank[:, s, :],
+                        lhsT=w4_q[t][0].bitcast(FP8X4),
+                        lhsT_scale=w4_q[t][1],
+                        rhs=h_codes[:, cols].bitcast(FP8X4),
+                        rhs_scale=h_scales[:, cols],
+                        start=True,
+                        stop=True,
+                    )
+                pair = slice(2 * u, 2 * u + 2)
+                if a == 0 and u == 0:
+                    nc.vector.tensor_copy(results[a][:, pair, :], bank[:])
+                else:
+                    nc.scalar.activation(results[a][:, pair, :], bank[:], COPY)
+                nc.sync.dma_start(out_rows[:, pair, cols], results[a][:, pair, :])
 
         y_codes = sb("y_codes", [P, V], U32)
         y_scales = sb("y_scales", [P, V], U8)
         codes_dram = out_1[0].rearrange("p n t -> p (n t)").bitcast(I32)
+        y_grouped = [sb("y_grouped%d" % a, [P, HALF * PACK], BF16) for a in range(2)]
+
+        def y_views(a):
+            src = results[a][:].rearrange("p t (g i) -> p g t i", i=4)
+            dst = y_grouped[a][:].rearrange("p (g i t) -> p g t i", i=4, t=PACK)
+            return dst, src
+
+        dst, src = y_views(0)
+        nc.vector.tensor_copy(dst, src)
+        dst, src = y_views(1)
+        nc.vector.tensor_copy(dst[:, :32], src[:, :32])
+        nc.scalar.activation(dst[:, 32:], src[:, 32:], COPY)
         for a in range(2):
             cols = slice(a * HALF, (a + 1) * HALF)
-            grouped = sb("y_grouped%d" % a, [P, HALF * PACK], BF16)
-            src = result[:, :, cols].rearrange("p t (g i) -> p g t i", i=4)
-            dst = grouped[:].rearrange("p (g i t) -> p g t i", i=4, t=PACK)
-            if a == 0:
-                nc.vector.tensor_copy(dst, src)
-            else:
-                nc.scalar.activation(dst, src, COPY)
-            quantize(nc, y_codes[:, cols], y_scales[:, cols], grouped[:])
+            quantize(nc, y_codes[:, cols], y_scales[:, cols], y_grouped[a][:])
             nc.sync.dma_start(codes_dram[:, cols], y_codes[:, cols].bitcast(I32))
         for q in range(4):
             queue = nc.sync if q % 2 == 0 else nc.scalar

@@ -51,20 +51,20 @@ def tile_picked_edgeup_relu_po_kernel(
         def load_halves(name, src):
             return [load_rows("%s%d" % (name, a), src[:, a * HALF : (a + 1) * HALF]) for a in range(2)]
 
-        w1_raw = [load_rows("w1_raw0", w1[:, :HALF])]
+        words_dram = x_words[0].rearrange("p n t -> p (n t)").bitcast(I32)
+        nc.sync.dma_start(node_words[:, : T // 2].bitcast(I32), words_dram[:, : T // 2])
         nc.sync.dma_start(offsets[:], offs)
         for q in range(4):
             nc.sync.dma_start(
                 node_scales[32 * q : 32 * q + 4, :].bitcast(I32),
                 x_scales[0][4 * q : 4 * q + 4, :].bitcast(I32),
             )
-        w1_raw.append(load_rows("w1_raw1", w1[:, HALF:]))
-        nc.sync.dma_start(node_words[:].bitcast(I32), x_words[0].rearrange("p n t -> p (n t)").bitcast(I32))
+        nc.sync.dma_start(node_words[:, T // 2 :].bitcast(I32), words_dram[:, T // 2 :])
         w3_raw = [load_rows("w3_raw", w3)]
-        w_raw = [w1_raw, load_halves("w2_raw", w2), w3_raw]
+        w_raw = [[load_rows("w1_raw", w1)], [load_rows("w2_raw", w2)], w3_raw]
         e_raw = load_halves("e_raw", eT)
         w_raw.append(load_halves("w4_raw", w4))
-        ON_VECTOR = {(2, 0, 1), (1, 1, 1), (3, 0, 0), (3, 0, 1), (3, 1, 1)}
+        ON_VECTOR = {(0, 0, 1), (1, 0, 1), (3, 0, 0), (3, 0, 1), (3, 1, 1)}
 
         end_scales = sb("end_scales", [P, S], U8)
         end_words = sb("end_words", [P, S], U32)
@@ -112,10 +112,10 @@ def tile_picked_edgeup_relu_po_kernel(
             for t in T_ORDER:
                 h_pass(c, t, weight, end_words[:, cols], end_scales[:, cols], side == 0 and t == T_ORDER[0], False)
 
+        w3_q = quantize_weight(2)
         w1_q = quantize_weight(0)
         for c in range(N_CHUNKS):
             node_passes(0, w1_q, c)
-        w3_q = quantize_weight(2)
         w2_q = quantize_weight(1)
 
         h_codes = sb("h_codes", [P, V], U32)

@@ -20,6 +20,7 @@ PACK = 4
 CHUNK = 128
 N_CHUNKS = V // CHUNK
 HALF = V // 2
+E_SPLIT = 22
 
 
 def quantize(nc, codes, scales, values):
@@ -64,7 +65,7 @@ def tile_picked_edgeup_relu_po_kernel(
         w_raw = [[load_rows("w1_raw", w1)], [load_rows("w2_raw", w2)], w3_raw]
         e_raw = load_halves("e_raw", eT)
         w_raw.append(load_halves("w4_raw", w4))
-        ON_VECTOR = {(0, 0, 1), (1, 0, 1), (3, 0, 0), (3, 0, 1), (3, 1, 1)}
+        ON_VECTOR = {0: (44, P), 1: (44, P), 2: (0, 0)}
 
         end_scales = sb("end_scales", [P, S], U8)
         end_words = sb("end_words", [P, S], U32)
@@ -79,10 +80,12 @@ def tile_picked_edgeup_relu_po_kernel(
                 m1 = m0 + src.shape[1]
                 for u in (1, 0):
                     dst = grouped[u][:].rearrange("p (t m j) -> p m j t", t=2, j=PACK)[:, m0:m1, :, :]
-                    if (i, n, u) not in ON_VECTOR:
-                        nc.scalar.activation(dst, src[:, :, :, 2 * u : 2 * u + 2], COPY)
-                    else:
-                        nc.vector.tensor_copy(dst, src[:, :, :, 2 * u : 2 * u + 2])
+                    pair = src[:, :, :, 2 * u : 2 * u + 2]
+                    split = ON_VECTOR[i][u]
+                    if split > 0:
+                        nc.vector.tensor_copy(dst[:, :split], pair[:, :split])
+                    if split < P:
+                        nc.scalar.activation(dst[:, split:], pair[:, split:], COPY)
                 m0 = m1
             parts = {}
             for u in (1, 0):
@@ -107,34 +110,57 @@ def tile_picked_edgeup_relu_po_kernel(
                 stop=stop,
             )
 
-        def node_passes(side, weight, c):
+        def node_passes(side, weight, c, stop):
             cols = slice(side * V + c * CHUNK, side * V + (c + 1) * CHUNK)
             for t in T_ORDER:
-                h_pass(c, t, weight, end_words[:, cols], end_scales[:, cols], side == 0 and t == T_ORDER[0], False)
+                h_pass(c, t, weight, end_words[:, cols], end_scales[:, cols], side == 0 and t == T_ORDER[0], stop and t == T_ORDER[-1])
 
         w3_q = quantize_weight(2)
         w1_q = quantize_weight(0)
         for c in range(N_CHUNKS):
-            node_passes(0, w1_q, c)
+            node_passes(0, w1_q, c, False)
         w2_q = quantize_weight(1)
 
         h_codes = sb("h_codes", [P, V], U32)
         h_scales = sb("h_scales", [P, V], U8)
 
-        def edge_half(a):
-            grouped = sb("e_grouped%d" % a, [P, HALF * PACK], BF16)
-            src = e_raw[a][:].rearrange("p j (g i) -> p g j i", i=4)
+        def edge_chunk(c):
+            a, s = divmod(c, 2)
+            grouped = sb("e_grouped%d" % c, [P, CHUNK * PACK], BF16)
+            src = e_raw[a][:, :, s * CHUNK : (s + 1) * CHUNK].rearrange("p j (g i) -> p g j i", i=4)
             dst = grouped[:].rearrange("p (g i j) -> p g j i", i=4, j=PACK)
-            nc.vector.tensor_copy(dst[:, :32], src[:, :32])
-            nc.scalar.activation(dst[:, 32:], src[:, 32:], COPY)
-            codes = sb("e_codes%d" % a, [P, HALF], U32)
-            scales = sb("e_scales%d" % a, [P, HALF], U8)
+            nc.vector.tensor_copy(dst[:, :E_SPLIT], src[:, :E_SPLIT])
+            nc.scalar.activation(dst[:, E_SPLIT:], src[:, E_SPLIT:], COPY)
+            return grouped
+
+        def edge_passes(c, grouped):
+            codes = sb("e_codes%d" % c, [P, CHUNK], U32)
+            scales = sb("e_scales%d" % c, [P, CHUNK], U8)
             quantize(nc, codes[:], scales[:], grouped[:])
+            if c == 0:
+                node_passes(1, w2_q, c, False)
+            for t in T_ORDER:
+                h_pass(c, t, w3_q, codes[:], scales[:], False, c == 0 and t == T_ORDER[-1])
+            if c > 0:
+                node_passes(1, w2_q, c, True)
+
+        def edge_half(a):
+            grouped = [edge_chunk(2 * a + s) for s in range(2)]
             for s in range(2):
-                c = 2 * a + s
-                cols = slice(s * CHUNK, (s + 1) * CHUNK)
-                for t in T_ORDER:
-                    h_pass(c, t, w3_q, codes[:, cols], scales[:, cols], False, t == T_ORDER[-1])
+                edge_passes(2 * a + s, grouped[s])
+
+        w4_codes = [sb("w4_codes%d" % t, [P, P], U32) for t in range(PACK)]
+        w4_scales = [sb("w4_scales%d" % t, [P, P], U8) for t in range(PACK)]
+
+        def w4_half(n):
+            src = w_raw[3][n][:].rearrange("p j (m t) -> p m j t", t=PACK)
+            grouped = [sb("w4_grouped%d_%d" % (n, u), [P, 2, HALF], BF16) for u in range(2)]
+            for u in range(2):
+                dst = grouped[u][:].rearrange("p t (m j) -> p m j t", j=PACK)
+                nc.vector.tensor_copy(dst, src[:, :, :, 2 * u : 2 * u + 2])
+            cols = slice(n * P // 2, (n + 1) * P // 2)
+            for t in range(PACK):
+                quantize(nc, w4_codes[t][:, cols], w4_scales[t][:, cols], grouped[t // 2][:, t % 2, :])
 
         out_banks = [psum.tile([P, 2, HALF], F32, name="out_bank%d" % n) for n in range(4)]
 
@@ -160,37 +186,47 @@ def tile_picked_edgeup_relu_po_kernel(
             quantize(nc, h_codes[:, cols], h_scales[:, cols], grouped[:])
 
         for a in range(2):
-            node_passes(1, w2_q, 2 * a)
-            node_passes(1, w2_q, 2 * a + 1)
             edge_half(a)
+        w4_half(0)
         hidden_half(0)
         warm(0, 4)
-        w4_q = quantize_weight(3)
+        w4_half(1)
         hidden_half(1)
 
         out_rows = out_0.rearrange("(p t) v -> p t v", t=PACK)
         results = [sb("result%d" % a, [P, PACK, HALF], F32) for a in range(2)]
-        for a in range(2):
+
+        def out_pass(dst, t, a):
             cols = slice(a * HALF, (a + 1) * HALF)
-            for u in (1, 0):
-                bank = out_banks[2 * a + u]
-                for s in range(2):
-                    t = 2 * u + s
-                    nc.tensor.matmul_mx(
-                        out=bank[:, s, :],
-                        lhsT=w4_q[t][0].bitcast(FP8X4),
-                        lhsT_scale=w4_q[t][1],
-                        rhs=h_codes[:, cols].bitcast(FP8X4),
-                        rhs_scale=h_scales[:, cols],
-                        start=True,
-                        stop=True,
-                    )
-                pair = slice(2 * u, 2 * u + 2)
-                if a == 0 and u == 0:
-                    nc.vector.tensor_copy(results[a][:, pair, :], bank[:])
-                else:
-                    nc.scalar.activation(results[a][:, pair, :], bank[:], COPY)
-                nc.sync.dma_start(out_rows[:, pair, cols], results[a][:, pair, :])
+            nc.tensor.matmul_mx(
+                out=dst,
+                lhsT=w4_codes[t][:].bitcast(FP8X4),
+                lhsT_scale=w4_scales[t][:],
+                rhs=h_codes[:, cols].bitcast(FP8X4),
+                rhs_scale=h_scales[:, cols],
+                start=True,
+                stop=True,
+            )
+
+        def empty(on_vector, dst, src):
+            if on_vector:
+                nc.vector.tensor_copy(dst, src)
+            else:
+                nc.scalar.activation(dst, src, COPY)
+
+        for t in range(PACK):
+            out_pass(out_banks[t][:, 0, :], t, 0)
+            empty(t % 2 == 1, results[0][:, t, :], out_banks[t][:, 0, :])
+            if t < 2:
+                nc.sync.dma_start(out_rows[:, t, :HALF], results[0][:, t, :])
+        nc.sync.dma_start(out_rows[:, 2:, :HALF], results[0][:, 2:, :])
+        late_banks = [psum.tile([P, 2, HALF], F32, name="h_bank%d" % u) for u in range(2)]
+        for u in range(2):
+            for s in range(2):
+                out_pass(late_banks[u][:, s, :], 2 * u + s, 1)
+            pair = slice(2 * u, 2 * u + 2)
+            empty(u == 1, results[1][:, pair, :], late_banks[u][:])
+            nc.sync.dma_start(out_rows[:, pair, HALF:], results[1][:, pair, :])
 
         y_codes = sb("y_codes", [P, V], U32)
         y_scales = sb("y_scales", [P, V], U8)
@@ -202,11 +238,10 @@ def tile_picked_edgeup_relu_po_kernel(
             dst = y_grouped[a][:].rearrange("p (g i t) -> p g t i", i=4, t=PACK)
             return dst, src
 
-        dst, src = y_views(0)
-        nc.vector.tensor_copy(dst, src)
-        dst, src = y_views(1)
-        nc.vector.tensor_copy(dst[:, :32], src[:, :32])
-        nc.scalar.activation(dst[:, 32:], src[:, 32:], COPY)
+        for a in range(2):
+            dst, src = y_views(a)
+            nc.vector.tensor_copy(dst[:, :32], src[:, :32])
+            nc.scalar.activation(dst[:, 32:], src[:, 32:], COPY)
         for a in range(2):
             cols = slice(a * HALF, (a + 1) * HALF)
             quantize(nc, y_codes[:, cols], y_scales[:, cols], y_grouped[a][:])

@@ -47,36 +47,45 @@ def tile_picked_edgeup_relu_po_kernel(
         def load_rows(name, src):
             raw = sb(name, [P, PACK, src.shape[1]], F32)
             nc.sync.dma_start(raw[:], src.rearrange("(p j) c -> p j c", j=PACK))
-            return raw
-
-        def load_halves(name, src):
-            return [load_rows("%s%d" % (name, a), src[:, a * HALF : (a + 1) * HALF]) for a in range(2)]
+            return raw[:]
 
         words_dram = x_words[0].rearrange("p n t -> p (n t)").bitcast(I32)
         nc.sync.dma_start(node_words[:, : T // 2].bitcast(I32), words_dram[:, : T // 2])
         nc.sync.dma_start(offsets[:], offs)
-        for q in range(4):
-            nc.sync.dma_start(
-                node_scales[32 * q : 32 * q + 4, :].bitcast(I32),
-                x_scales[0][4 * q : 4 * q + 4, :].bitcast(I32),
-            )
+        nc.sync.dma_start(node_scales[4:P:8, :].bitcast(I32), x_scales[0].bitcast(I32))
         nc.sync.dma_start(node_words[:, T // 2 :].bitcast(I32), words_dram[:, T // 2 :])
-        w3_raw = [load_rows("w3_raw", w3)]
-        w_raw = [[load_rows("w1_raw", w1)], [load_rows("w2_raw", w2)], w3_raw]
-        e_raw = load_halves("e_raw", eT)
-        w_raw.append(load_halves("w4_raw", w4))
+        w3_raw = load_rows("w3_raw", w3)
+        w1_raw = load_rows("w1_raw", w1)
         ON_VECTOR = {0: (44, P), 1: (44, P), 2: (0, 0)}
 
+        picked_scales = sb("picked_scales", [P, S], U8)
         end_scales = sb("end_scales", [P, S], U8)
+        nc.vector.memset(end_scales[:].bitcast(I32), 0)
         end_words = sb("end_words", [P, S], U32)
-        nc.vector.tensor_copy(end_scales[:], node_scales[:].indirect(offsets[:]))
+        nc.vector.tensor_copy(picked_scales[:], node_scales[:].indirect(offsets[:]))
+        for r in range(4):
+            nc.sync.dma_start(
+                end_scales[r:P:32, :].bitcast(I32),
+                picked_scales[8 * r + 4 : P : 32, :].bitcast(I32),
+            )
+        late = sb("node_scales", [P, 3 * PACK * H], F32)
+
+        def load_late(first, src):
+            width = src.shape[1]
+            raw = late[:, first : first + PACK * width].rearrange("p (j c) -> p j c", j=PACK)
+            nc.sync.dma_start(raw, src.rearrange("(p j) c -> p j c", j=PACK))
+            return raw
+
+        w_raw = [[w1_raw], [load_late(0, w2)], [w3_raw]]
+        e_raw = [load_late(PACK * (H + a * HALF), eT[:, a * HALF : (a + 1) * HALF]) for a in range(2)]
+        w_raw.append([load_late(PACK * (H + V + a * HALF), w4[:, a * HALF : (a + 1) * HALF]) for a in range(2)])
         nc.vector.tensor_copy(end_words[:], node_words[:].indirect(offsets[:]))
 
         def quantize_weight(i):
             grouped = [sb("w%d_grouped%d" % (i, u), [P, 2 * P * PACK], BF16) for u in range(2)]
             m0 = 0
             for n, raw in enumerate(w_raw[i]):
-                src = raw[:].rearrange("p j (m t) -> p m j t", t=PACK)
+                src = raw.rearrange("p j (m t) -> p m j t", t=PACK)
                 m1 = m0 + src.shape[1]
                 for u in (1, 0):
                     dst = grouped[u][:].rearrange("p (t m j) -> p m j t", t=2, j=PACK)[:, m0:m1, :, :]
@@ -153,7 +162,7 @@ def tile_picked_edgeup_relu_po_kernel(
         w4_scales = [sb("w4_scales%d" % t, [P, P], U8) for t in range(PACK)]
 
         def w4_half(n):
-            src = w_raw[3][n][:].rearrange("p j (m t) -> p m j t", t=PACK)
+            src = w_raw[3][n].rearrange("p j (m t) -> p m j t", t=PACK)
             grouped = [sb("w4_grouped%d_%d" % (n, u), [P, 2, HALF], BF16) for u in range(2)]
             for u in range(2):
                 dst = grouped[u][:].rearrange("p t (m j) -> p m j t", j=PACK)

@@ -205,8 +205,7 @@ def tile_picked_edgeup_relu_po_kernel(
         out_rows = out_0.rearrange("(p t) v -> p t v", t=PACK)
         results = [sb("result%d" % a, [P, PACK, HALF], F32) for a in range(2)]
 
-        def out_pass(dst, t, a):
-            cols = slice(a * HALF, (a + 1) * HALF)
+        def out_pass(dst, t, cols):
             nc.tensor.matmul_mx(
                 out=dst,
                 lhsT=w4_codes[t][:].bitcast(FP8X4),
@@ -223,19 +222,26 @@ def tile_picked_edgeup_relu_po_kernel(
             else:
                 nc.scalar.activation(dst, src, COPY)
 
-        for t in range(PACK):
-            out_pass(out_banks[t][:, 0, :], t, 0)
-            empty(t % 2 == 1, results[0][:, t, :], out_banks[t][:, 0, :])
-            if t < 2:
+        for c in range(2):
+            cols = slice(c * CHUNK, (c + 1) * CHUNK)
+            out_pass(out_banks[c][:, 0, :CHUNK], 0, cols)
+            empty(c == 1, results[0][:, 0, cols], out_banks[c][:, 0, :CHUNK])
+        nc.sync.dma_start(out_rows[:, 0, :HALF], results[0][:, 0, :])
+        late_banks = [psum.tile([P, 2, HALF], F32, name="h_bank%d" % u) for u in range(4)]
+        for t, bank in ((1, out_banks[2]), (2, out_banks[3]), (3, late_banks[0])):
+            out_pass(bank[:, 0, :], t, slice(0, HALF))
+            empty(t == 2, results[0][:, t, :], bank[:, 0, :])
+            if t == 1:
                 nc.sync.dma_start(out_rows[:, t, :HALF], results[0][:, t, :])
         nc.sync.dma_start(out_rows[:, 2:, :HALF], results[0][:, 2:, :])
-        late_banks = [psum.tile([P, 2, HALF], F32, name="h_bank%d" % u) for u in range(2)]
-        for u in range(2):
-            for s in range(2):
-                out_pass(late_banks[u][:, s, :], 2 * u + s, 1)
-            pair = slice(2 * u, 2 * u + 2)
-            empty(u == 1, results[1][:, pair, :], late_banks[u][:])
-            nc.sync.dma_start(out_rows[:, pair, HALF:], results[1][:, pair, :])
+        for s in range(2):
+            out_pass(late_banks[1][:, s, :], s, slice(HALF, V))
+        empty(False, results[1][:, :2, :], late_banks[1][:])
+        nc.sync.dma_start(out_rows[:, :2, HALF:], results[1][:, :2, :])
+        for t in (2, 3):
+            out_pass(late_banks[t][:, 0, :], t, slice(HALF, V))
+            empty(t == 2, results[1][:, t, :], late_banks[t][:, 0, :])
+        nc.sync.dma_start(out_rows[:, 2:, HALF:], results[1][:, 2:, :])
 
         y_codes = sb("y_codes", [P, V], U32)
         y_scales = sb("y_scales", [P, V], U8)
@@ -247,14 +253,17 @@ def tile_picked_edgeup_relu_po_kernel(
             dst = y_grouped[a][:].rearrange("p (g i t) -> p g t i", i=4, t=PACK)
             return dst, src
 
-        for a in range(2):
-            dst, src = y_views(a)
-            nc.vector.tensor_copy(dst[:, :32], src[:, :32])
-            nc.scalar.activation(dst[:, 32:], src[:, 32:], COPY)
-        for a in range(2):
-            cols = slice(a * HALF, (a + 1) * HALF)
-            quantize(nc, y_codes[:, cols], y_scales[:, cols], y_grouped[a][:])
-            nc.sync.dma_start(codes_dram[:, cols], y_codes[:, cols].bitcast(I32))
+        dst, src = y_views(0)
+        nc.vector.tensor_copy(dst, src)
+        dst, src = y_views(1)
+        nc.vector.tensor_copy(dst[:, :32], src[:, :32])
+        nc.scalar.activation(dst[:, 32:], src[:, 32:], COPY)
+        quantize(nc, y_codes[:, :HALF], y_scales[:, :HALF], y_grouped[0][:])
+        nc.sync.dma_start(codes_dram[:, :HALF], y_codes[:, :HALF].bitcast(I32))
+        for s in range(2):
+            cols = slice(HALF + s * CHUNK, HALF + (s + 1) * CHUNK)
+            quantize(nc, y_codes[:, cols], y_scales[:, cols], y_grouped[1][:, s * CHUNK * PACK : (s + 1) * CHUNK * PACK])
+        nc.sync.dma_start(codes_dram[:, HALF:], y_codes[:, HALF:].bitcast(I32))
         for q in range(4):
             queue = nc.sync if q % 2 == 0 else nc.scalar
             queue.dma_start(

@@ -12,7 +12,6 @@ I32 = mybir.dt.int32
 U16 = mybir.dt.uint16
 U8 = mybir.dt.uint8
 FP8X4 = mybir.dt.float8_e4m3fn_x4
-COPY = mybir.ActivationFunctionType.Copy
 RELU = mybir.ActivationFunctionType.Relu
 
 P = 128
@@ -94,7 +93,7 @@ def tile_picked_edgeup_relu_po_kernel(
                     if split > 0:
                         nc.vector.tensor_copy(dst[:, :split], pair[:, :split])
                     if split < P:
-                        nc.scalar.activation(dst[:, split:], pair[:, split:], COPY)
+                        nc.scalar.copy(dst[:, split:], pair[:, split:])
                 m0 = m1
             parts = {}
             for u in (1, 0):
@@ -139,7 +138,7 @@ def tile_picked_edgeup_relu_po_kernel(
             src = e_raw[a][:, :, s * CHUNK : (s + 1) * CHUNK].rearrange("p j (g i) -> p g j i", i=4)
             dst = grouped[:].rearrange("p (g i j) -> p g j i", i=4, j=PACK)
             nc.vector.tensor_copy(dst[:, :E_SPLIT], src[:, :E_SPLIT])
-            nc.scalar.activation(dst[:, E_SPLIT:], src[:, E_SPLIT:], COPY)
+            nc.scalar.copy(dst[:, E_SPLIT:], src[:, E_SPLIT:])
             return grouped
 
         def edge_passes(c, grouped):
@@ -220,7 +219,7 @@ def tile_picked_edgeup_relu_po_kernel(
             if on_vector:
                 nc.vector.tensor_copy(dst, src)
             else:
-                nc.scalar.activation(dst, src, COPY)
+                nc.scalar.copy(dst, src)
 
         for c in range(2):
             cols = slice(c * CHUNK, (c + 1) * CHUNK)
@@ -257,7 +256,7 @@ def tile_picked_edgeup_relu_po_kernel(
         nc.vector.tensor_copy(dst, src)
         dst, src = y_views(1)
         nc.vector.tensor_copy(dst[:, :32], src[:, :32])
-        nc.scalar.activation(dst[:, 32:], src[:, 32:], COPY)
+        nc.scalar.copy(dst[:, 32:], src[:, 32:])
         quantize(nc, y_codes[:, :HALF], y_scales[:, :HALF], y_grouped[0][:])
         nc.sync.dma_start(codes_dram[:, :HALF], y_codes[:, :HALF].bitcast(I32))
         for s in range(2):

@@ -100,6 +100,7 @@ def tile_picked_edgeup_relu_po_kernel(
                 codes = sb("w%d_codes%d" % (i, u), [P, 2 * P], U32)
                 scales = sb("w%d_scales%d" % (i, u), [P, 2 * P], U8)
                 quantize(nc, codes[:], scales[:], grouped[u][:])
+                parts["pair%d" % u] = (codes[:], scales[:])
                 for s in range(2):
                     parts[2 * u + s] = (codes[:, s * P : (s + 1) * P], scales[:, s * P : (s + 1) * P])
             return parts
@@ -123,7 +124,22 @@ def tile_picked_edgeup_relu_po_kernel(
             for t in T_ORDER:
                 h_pass(c, t, weight, end_words[:, cols], end_scales[:, cols], side == 0 and t == T_ORDER[0], stop and t == T_ORDER[-1])
 
+        out_banks = [psum.tile([P, 2, HALF], F32, name="out_bank%d" % n) for n in range(4)]
+
+        def warm(count, codes, scales, moving, moving_scales):
+            for n in range(count):
+                nc.tensor.matmul_mx(
+                    out=out_banks[n][:].rearrange("p s v -> p (s v)")[:, : moving.shape[1]],
+                    lhsT=codes.bitcast(FP8X4),
+                    lhsT_scale=scales,
+                    rhs=moving.bitcast(FP8X4),
+                    rhs_scale=moving_scales,
+                    start=True,
+                    stop=True,
+                )
+
         w3_q = quantize_weight(2)
+        warm(3, *w3_q[2], *w3_q["pair1"])
         w1_q = quantize_weight(0)
         for c in range(N_CHUNKS):
             node_passes(0, w1_q, c, False)
@@ -170,21 +186,6 @@ def tile_picked_edgeup_relu_po_kernel(
             for t in range(PACK):
                 quantize(nc, w4_codes[t][:, cols], w4_scales[t][:, cols], grouped[t // 2][:, t % 2, :])
 
-        out_banks = [psum.tile([P, 2, HALF], F32, name="out_bank%d" % n) for n in range(4)]
-
-        def warm(first, count):
-            cols = slice(first, first + HALF)
-            for n in range(count):
-                nc.tensor.matmul_mx(
-                    out=out_banks[n][:, 0, :],
-                    lhsT=w3_q[n][0].bitcast(FP8X4),
-                    lhsT_scale=w3_q[n][1],
-                    rhs=h_codes[:, cols].bitcast(FP8X4),
-                    rhs_scale=h_scales[:, cols],
-                    start=True,
-                    stop=True,
-                )
-
         def hidden_half(a):
             grouped = sb("h_grouped%d" % a, [P, HALF * PACK], BF16)
             for s in range(2):
@@ -197,7 +198,7 @@ def tile_picked_edgeup_relu_po_kernel(
             edge_half(a)
         w4_half(0)
         hidden_half(0)
-        warm(0, 4)
+        warm(2, h_codes[:, :P], h_scales[:, :P], end_words[:, :V], end_scales[:, :V])
         w4_half(1)
         hidden_half(1)
 

@@ -51,7 +51,7 @@ def tile_picked_edgeup_relu_po_kernel(
         words_dram = x_words[0].rearrange("p n t -> p (n t)").bitcast(I32)
         nc.sync.dma_start(node_words[:, : T // 2].bitcast(I32), words_dram[:, : T // 2])
         nc.sync.dma_start(offsets[:], offs)
-        nc.sync.dma_start(node_scales[4:P:8, :].bitcast(I32), x_scales[0].bitcast(I32))
+        nc.sync.dma_start(node_scales[0:P:8, :].bitcast(I32), x_scales[0].bitcast(I32))
         nc.sync.dma_start(node_words[:, T // 2 :].bitcast(I32), words_dram[:, T // 2 :])
         w3_raw = load_rows("w3_raw", w3)
         w1_raw = load_rows("w1_raw", w1)
@@ -59,13 +59,13 @@ def tile_picked_edgeup_relu_po_kernel(
 
         picked_scales = sb("picked_scales", [P, S], U8)
         end_scales = sb("end_scales", [P, S], U8)
-        nc.vector.memset(end_scales[:].bitcast(I32), 0)
         end_words = sb("end_words", [P, S], U32)
         nc.vector.tensor_copy(picked_scales[:], node_scales[:].indirect(offsets[:]))
-        for r in range(4):
+        nc.vector.tensor_copy(end_scales[:].bitcast(I32), picked_scales[:].bitcast(I32))
+        for r in range(1, 4):
             nc.sync.dma_start(
                 end_scales[r:P:32, :].bitcast(I32),
-                picked_scales[8 * r + 4 : P : 32, :].bitcast(I32),
+                picked_scales[8 * r : P : 32, :].bitcast(I32),
             )
         late = sb("node_scales", [P, 3 * PACK * H], F32)
 
@@ -237,11 +237,10 @@ def tile_picked_edgeup_relu_po_kernel(
         for s in range(2):
             out_pass(late_banks[1][:, s, :], s, slice(HALF, V))
         empty(False, results[1][:, :2, :], late_banks[1][:])
-        nc.sync.dma_start(out_rows[:, :2, HALF:], results[1][:, :2, :])
         for t in (2, 3):
             out_pass(late_banks[t][:, 0, :], t, slice(HALF, V))
             empty(t == 2, results[1][:, t, :], late_banks[t][:, 0, :])
-        nc.sync.dma_start(out_rows[:, 2:, HALF:], results[1][:, 2:, :])
+        nc.sync.dma_start(out_rows[:, :, HALF:], results[1][:])
 
         y_codes = sb("y_codes", [P, V], U32)
         y_scales = sb("y_scales", [P, V], U8)

@@ -20,6 +20,7 @@ CHUNK = 128
 N_CHUNKS = V // CHUNK
 HALF = V // 2
 E_SPLIT = 22
+Y_SPLIT = 24
 
 
 def quantize(nc, codes, scales, values):
@@ -161,11 +162,11 @@ def tile_picked_edgeup_relu_po_kernel(
             codes = sb("e_codes%d" % c, [P, CHUNK], U32)
             scales = sb("e_scales%d" % c, [P, CHUNK], U8)
             quantize(nc, codes[:], scales[:], grouped[:])
-            if c == 0:
+            if c % 2 == 0:
                 node_passes(1, w2_q, c, False)
             for t in T_ORDER:
-                h_pass(c, t, w3_q, codes[:], scales[:], False, c == 0 and t == T_ORDER[-1])
-            if c > 0:
+                h_pass(c, t, w3_q, codes[:], scales[:], False, c % 2 == 0 and t == T_ORDER[-1])
+            if c % 2 == 1:
                 node_passes(1, w2_q, c, True)
 
         def edge_half(a):
@@ -176,15 +177,17 @@ def tile_picked_edgeup_relu_po_kernel(
         w4_codes = [sb("w4_codes%d" % t, [P, P], U32) for t in range(PACK)]
         w4_scales = [sb("w4_scales%d" % t, [P, P], U8) for t in range(PACK)]
 
-        def w4_half(n):
+        w4_grouped = [sb("w4_grouped%d" % u, [P, 2, H], BF16) for u in range(2)]
+
+        def round_w4(n):
             src = w_raw[3][n].rearrange("p j (m t) -> p m j t", t=PACK)
-            grouped = [sb("w4_grouped%d_%d" % (n, u), [P, 2, HALF], BF16) for u in range(2)]
             for u in range(2):
-                dst = grouped[u][:].rearrange("p t (m j) -> p m j t", j=PACK)
+                dst = w4_grouped[u][:].rearrange("p t (m j) -> p m j t", j=PACK)[:, n * P // 2 : (n + 1) * P // 2]
                 nc.vector.tensor_copy(dst, src[:, :, :, 2 * u : 2 * u + 2])
-            cols = slice(n * P // 2, (n + 1) * P // 2)
-            for t in range(PACK):
-                quantize(nc, w4_codes[t][:, cols], w4_scales[t][:, cols], grouped[t // 2][:, t % 2, :])
+
+        def quantize_w4(t, first, last):
+            values = w4_grouped[t // 2][:, t % 2, first * PACK : last * PACK]
+            quantize(nc, w4_codes[t][:, first:last], w4_scales[t][:, first:last], values)
 
         def hidden_half(a):
             grouped = sb("h_grouped%d" % a, [P, HALF * PACK], BF16)
@@ -196,51 +199,50 @@ def tile_picked_edgeup_relu_po_kernel(
 
         for a in range(2):
             edge_half(a)
-        w4_half(0)
+        round_w4(0)
+        for t in range(2):
+            quantize_w4(t, 0, P // 2)
         hidden_half(0)
         warm(2, h_codes[:, :P], h_scales[:, :P], end_words[:, :V], end_scales[:, :V])
-        w4_half(1)
+        round_w4(1)
+        for t in range(2):
+            quantize_w4(t, P // 2, P)
         hidden_half(1)
+        for t in (2, 3):
+            quantize_w4(t, 0, P)
 
         out_rows = out_0.rearrange("(p t) v -> p t v", t=PACK)
-        results = [sb("result%d" % a, [P, PACK, HALF], F32) for a in range(2)]
+        result = sb("result", [P, PACK, V], F32)
 
-        def out_pass(dst, t, cols):
-            nc.tensor.matmul_mx(
-                out=dst,
-                lhsT=w4_codes[t][:].bitcast(FP8X4),
-                lhsT_scale=w4_scales[t][:],
-                rhs=h_codes[:, cols].bitcast(FP8X4),
-                rhs_scale=h_scales[:, cols],
-                start=True,
-                stop=True,
-            )
-
-        def empty(on_vector, dst, src):
+        def out_slices(bank, ts, a, on_vector):
+            cols = slice(a * HALF, (a + 1) * HALF)
+            for s, t in enumerate(ts):
+                nc.tensor.matmul_mx(
+                    out=bank[:, s, :],
+                    lhsT=w4_codes[t][:].bitcast(FP8X4),
+                    lhsT_scale=w4_scales[t][:],
+                    rhs=h_codes[:, cols].bitcast(FP8X4),
+                    rhs_scale=h_scales[:, cols],
+                    start=True,
+                    stop=True,
+                )
+            dst = result[:, ts[0] : ts[-1] + 1, cols]
             if on_vector:
-                nc.vector.tensor_copy(dst, src)
+                nc.vector.tensor_copy(dst, bank[:, : len(ts), :])
             else:
-                nc.scalar.copy(dst, src)
+                nc.scalar.copy(dst, bank[:, : len(ts), :])
 
-        for c in range(2):
-            cols = slice(c * CHUNK, (c + 1) * CHUNK)
-            out_pass(out_banks[c][:, 0, :CHUNK], 0, cols)
-            empty(c == 1, results[0][:, 0, cols], out_banks[c][:, 0, :CHUNK])
-        nc.sync.dma_start(out_rows[:, 0, :HALF], results[0][:, 0, :])
-        late_banks = [psum.tile([P, 2, HALF], F32, name="h_bank%d" % u) for u in range(4)]
-        for t, bank in ((1, out_banks[2]), (2, out_banks[3]), (3, late_banks[0])):
-            out_pass(bank[:, 0, :], t, slice(0, HALF))
-            empty(t == 2, results[0][:, t, :], bank[:, 0, :])
-            if t == 1:
-                nc.sync.dma_start(out_rows[:, t, :HALF], results[0][:, t, :])
-        nc.sync.dma_start(out_rows[:, 2:, :HALF], results[0][:, 2:, :])
-        for s in range(2):
-            out_pass(late_banks[1][:, s, :], s, slice(HALF, V))
-        empty(False, results[1][:, :2, :], late_banks[1][:])
-        for t in (2, 3):
-            out_pass(late_banks[t][:, 0, :], t, slice(HALF, V))
-            empty(t == 2, results[1][:, t, :], late_banks[t][:, 0, :])
-        nc.sync.dma_start(out_rows[:, :, HALF:], results[1][:])
+        late_banks = [psum.tile([P, 2, HALF], F32, name="h_bank%d" % u) for u in range(3)]
+        for t in range(2):
+            out_slices(out_banks[2 + t], (t,), 0, False)
+            nc.sync.dma_start(out_rows[:, t, :HALF], result[:, t, :HALF])
+        out_slices(out_banks[0], (0, 1), 1, False)
+        nc.sync.dma_start(out_rows[:, :2, HALF:], result[:, :2, HALF:])
+        out_slices(out_banks[1], (2,), 0, True)
+        out_slices(late_banks[0], (3,), 0, True)
+        out_slices(late_banks[1], (2,), 1, False)
+        out_slices(late_banks[2], (3,), 1, True)
+        nc.sync.dma_start(out_rows[:, 2:, :], result[:, 2:, :])
 
         y_codes = sb("y_codes", [P, V], U32)
         y_scales = sb("y_scales", [P, V], U8)
@@ -248,21 +250,19 @@ def tile_picked_edgeup_relu_po_kernel(
         y_grouped = [sb("y_grouped%d" % a, [P, HALF * PACK], BF16) for a in range(2)]
 
         def y_views(a):
-            src = results[a][:].rearrange("p t (g i) -> p g t i", i=4)
+            src = result[:, :, a * HALF : (a + 1) * HALF].rearrange("p t (g i) -> p g t i", i=4)
             dst = y_grouped[a][:].rearrange("p (g i t) -> p g t i", i=4, t=PACK)
             return dst, src
 
         dst, src = y_views(0)
         nc.vector.tensor_copy(dst, src)
         dst, src = y_views(1)
-        nc.vector.tensor_copy(dst[:, :32], src[:, :32])
-        nc.scalar.copy(dst[:, 32:], src[:, 32:])
-        quantize(nc, y_codes[:, :HALF], y_scales[:, :HALF], y_grouped[0][:])
-        nc.sync.dma_start(codes_dram[:, :HALF], y_codes[:, :HALF].bitcast(I32))
-        for s in range(2):
-            cols = slice(HALF + s * CHUNK, HALF + (s + 1) * CHUNK)
-            quantize(nc, y_codes[:, cols], y_scales[:, cols], y_grouped[1][:, s * CHUNK * PACK : (s + 1) * CHUNK * PACK])
-        nc.sync.dma_start(codes_dram[:, HALF:], y_codes[:, HALF:].bitcast(I32))
+        nc.vector.tensor_copy(dst[:, :Y_SPLIT], src[:, :Y_SPLIT])
+        nc.scalar.copy(dst[:, Y_SPLIT:], src[:, Y_SPLIT:])
+        for a in range(2):
+            cols = slice(a * HALF, (a + 1) * HALF)
+            quantize(nc, y_codes[:, cols], y_scales[:, cols], y_grouped[a][:])
+            nc.sync.dma_start(codes_dram[:, cols], y_codes[:, cols].bitcast(I32))
         for q in range(4):
             queue = nc.sync if q % 2 == 0 else nc.scalar
             queue.dma_start(

@@ -36,7 +36,7 @@ def tile_picked_edgeup_relu_po_kernel(
         psum = ctx.enter_context(tc.psum_pool(name="psum", bufs=1))
 
         def sb(name, shape, dtype):
-            return keep.tile(shape, dtype, name=name, align_bytes=64)
+            return keep.tile(shape, dtype, name=name, align_bytes=256)
 
         offsets = keep.tile([P, S // 16], U16, name="offsets")
         node_words = sb("node_words", [P, T], U32)

@@ -50,11 +50,11 @@ def tile_picked_edgeup_relu_po_kernel(
             return raw[:]
 
         words_dram = x_words[0].rearrange("p n t -> p (n t)").bitcast(I32)
-        nc.sync.dma_start(node_words[:, : T // 2].bitcast(I32), words_dram[:, : T // 2])
+        w3_raw = [load_rows("w3_raw0", w3[:, :HALF])]
         nc.sync.dma_start(offsets[:], offs)
         nc.sync.dma_start(node_scales[0:P:8, :].bitcast(I32), x_scales[0].bitcast(I32))
-        nc.sync.dma_start(node_words[:, T // 2 :].bitcast(I32), words_dram[:, T // 2 :])
-        w3_raw = load_rows("w3_raw", w3)
+        w3_raw.append(load_rows("w3_raw1", w3[:, HALF:]))
+        nc.sync.dma_start(node_words[:].bitcast(I32), words_dram)
         w1_raw = load_rows("w1_raw", w1)
         ON_VECTOR = {0: (44, P), 1: (44, P), 2: (0, 0)}
 
@@ -76,10 +76,9 @@ def tile_picked_edgeup_relu_po_kernel(
             nc.sync.dma_start(raw, src.rearrange("(p j) c -> p j c", j=PACK))
             return raw
 
-        w_raw = [[w1_raw], [load_late(0, w2)], [w3_raw]]
+        w_raw = [[w1_raw], [load_late(0, w2)], w3_raw]
         e_raw = [load_late(PACK * (H + a * HALF), eT[:, a * HALF : (a + 1) * HALF]) for a in range(2)]
         w_raw.append([load_late(PACK * (H + V + a * HALF), w4[:, a * HALF : (a + 1) * HALF]) for a in range(2)])
-        nc.vector.tensor_copy(end_words[:], node_words[:].indirect(offsets[:]))
 
         def quantize_weight(i):
             grouped = [sb("w%d_grouped%d" % (i, u), [P, 2 * P * PACK], BF16) for u in range(2)]
@@ -93,7 +92,7 @@ def tile_picked_edgeup_relu_po_kernel(
                     split = ON_VECTOR[i][u]
                     if split > 0:
                         nc.vector.tensor_copy(dst[:, :split], pair[:, :split])
-                    if split < P:
+                    if split < m1 - m0:
                         nc.scalar.copy(dst[:, split:], pair[:, split:])
                 m0 = m1
             parts = {}
@@ -101,7 +100,6 @@ def tile_picked_edgeup_relu_po_kernel(
                 codes = sb("w%d_codes%d" % (i, u), [P, 2 * P], U32)
                 scales = sb("w%d_scales%d" % (i, u), [P, 2 * P], U8)
                 quantize(nc, codes[:], scales[:], grouped[u][:])
-                parts["pair%d" % u] = (codes[:], scales[:])
                 for s in range(2):
                     parts[2 * u + s] = (codes[:, s * P : (s + 1) * P], scales[:, s * P : (s + 1) * P])
             return parts
@@ -140,7 +138,7 @@ def tile_picked_edgeup_relu_po_kernel(
                 )
 
         w3_q = quantize_weight(2)
-        warm(3, *w3_q[2], *w3_q["pair1"])
+        nc.vector.tensor_copy(end_words[:], node_words[:].indirect(offsets[:]))
         w1_q = quantize_weight(0)
         for c in range(N_CHUNKS):
             node_passes(0, w1_q, c, False)
@@ -203,7 +201,7 @@ def tile_picked_edgeup_relu_po_kernel(
         for t in range(2):
             quantize_w4(t, 0, P // 2)
         hidden_half(0)
-        warm(2, h_codes[:, :P], h_scales[:, :P], end_words[:, :V], end_scales[:, :V])
+        warm(3, h_codes[:, :P], h_scales[:, :P], h_codes[:, :HALF], h_scales[:, :HALF])
         round_w4(1)
         for t in range(2):
             quantize_w4(t, P // 2, P)

@@ -19,7 +19,7 @@ PACK = 4
 CHUNK = 128
 N_CHUNKS = V // CHUNK
 HALF = V // 2
-E_SPLIT = 22
+E_SPLIT = (0, 0, 32, 32)
 Y_SPLIT = 24
 
 
@@ -50,13 +50,13 @@ def tile_picked_edgeup_relu_po_kernel(
             return raw[:]
 
         words_dram = x_words[0].rearrange("p n t -> p (n t)").bitcast(I32)
-        w3_raw = [load_rows("w3_raw0", w3[:, :HALF])]
+        nc.sync.dma_start(node_words[:, : T // 2].bitcast(I32), words_dram[:, : T // 2])
         nc.sync.dma_start(offsets[:], offs)
         nc.sync.dma_start(node_scales[0:P:8, :].bitcast(I32), x_scales[0].bitcast(I32))
-        w3_raw.append(load_rows("w3_raw1", w3[:, HALF:]))
-        nc.sync.dma_start(node_words[:].bitcast(I32), words_dram)
+        nc.sync.dma_start(node_words[:, T // 2 :].bitcast(I32), words_dram[:, T // 2 :])
         w1_raw = load_rows("w1_raw", w1)
-        ON_VECTOR = {0: (44, P), 1: (44, P), 2: (0, 0)}
+        w2_raw = load_rows("w2_raw", w2)
+        ON_VECTOR = {0: (96, 0), 1: (P, 0), 2: (44, P)}
 
         picked_scales = sb("picked_scales", [P, S], U8)
         end_scales = sb("end_scales", [P, S], U8)
@@ -76,12 +76,15 @@ def tile_picked_edgeup_relu_po_kernel(
             nc.sync.dma_start(raw, src.rearrange("(p j) c -> p j c", j=PACK))
             return raw
 
-        w_raw = [[w1_raw], [load_late(0, w2)], w3_raw]
+        w_raw = [[w1_raw], [w2_raw], [load_late(0, w3)]]
         e_raw = [load_late(PACK * (H + a * HALF), eT[:, a * HALF : (a + 1) * HALF]) for a in range(2)]
         w_raw.append([load_late(PACK * (H + V + a * HALF), w4[:, a * HALF : (a + 1) * HALF]) for a in range(2)])
 
         def quantize_weight(i):
-            grouped = [sb("w%d_grouped%d" % (i, u), [P, 2 * P * PACK], BF16) for u in range(2)]
+            names = ["w%d_grouped%d" % (i, u) for u in range(2)]
+            if i == 1:
+                names[0] = "w0_grouped0"
+            grouped = [sb(name, [P, 2 * P * PACK], BF16) for name in names]
             m0 = 0
             for n, raw in enumerate(w_raw[i]):
                 src = raw.rearrange("p j (m t) -> p m j t", t=PACK)
@@ -92,7 +95,7 @@ def tile_picked_edgeup_relu_po_kernel(
                     split = ON_VECTOR[i][u]
                     if split > 0:
                         nc.vector.tensor_copy(dst[:, :split], pair[:, :split])
-                    if split < m1 - m0:
+                    if split < P:
                         nc.scalar.copy(dst[:, split:], pair[:, split:])
                 m0 = m1
             parts = {}
@@ -118,10 +121,12 @@ def tile_picked_edgeup_relu_po_kernel(
                 stop=stop,
             )
 
-        def node_passes(side, weight, c, stop):
-            cols = slice(side * V + c * CHUNK, side * V + (c + 1) * CHUNK)
-            for t in T_ORDER:
-                h_pass(c, t, weight, end_words[:, cols], end_scales[:, cols], side == 0 and t == T_ORDER[0], stop and t == T_ORDER[-1])
+        def node_passes(side, weight):
+            for ts in (T_ORDER[:2], T_ORDER[2:]):
+                for c in range(N_CHUNKS):
+                    cols = slice(side * V + c * CHUNK, side * V + (c + 1) * CHUNK)
+                    for t in ts:
+                        h_pass(c, t, weight, end_words[:, cols], end_scales[:, cols], side == 0 and t == T_ORDER[0], False)
 
         out_banks = [psum.tile([P, 2, HALF], F32, name="out_bank%d" % n) for n in range(4)]
 
@@ -137,12 +142,11 @@ def tile_picked_edgeup_relu_po_kernel(
                     stop=True,
                 )
 
-        w3_q = quantize_weight(2)
         nc.vector.tensor_copy(end_words[:], node_words[:].indirect(offsets[:]))
         w1_q = quantize_weight(0)
-        for c in range(N_CHUNKS):
-            node_passes(0, w1_q, c, False)
-        w2_q = quantize_weight(1)
+        node_passes(0, w1_q)
+        node_passes(1, quantize_weight(1))
+        w3_q = quantize_weight(2)
 
         h_codes = sb("h_codes", [P, V], U32)
         h_scales = sb("h_scales", [P, V], U8)
@@ -152,20 +156,18 @@ def tile_picked_edgeup_relu_po_kernel(
             grouped = sb("e_grouped%d" % c, [P, CHUNK * PACK], BF16)
             src = e_raw[a][:, :, s * CHUNK : (s + 1) * CHUNK].rearrange("p j (g i) -> p g j i", i=4)
             dst = grouped[:].rearrange("p (g i j) -> p g j i", i=4, j=PACK)
-            nc.vector.tensor_copy(dst[:, :E_SPLIT], src[:, :E_SPLIT])
-            nc.scalar.copy(dst[:, E_SPLIT:], src[:, E_SPLIT:])
+            if E_SPLIT[c] > 0:
+                nc.vector.tensor_copy(dst[:, : E_SPLIT[c]], src[:, : E_SPLIT[c]])
+            if E_SPLIT[c] < CHUNK // 4:
+                nc.scalar.copy(dst[:, E_SPLIT[c] :], src[:, E_SPLIT[c] :])
             return grouped
 
         def edge_passes(c, grouped):
             codes = sb("e_codes%d" % c, [P, CHUNK], U32)
             scales = sb("e_scales%d" % c, [P, CHUNK], U8)
             quantize(nc, codes[:], scales[:], grouped[:])
-            if c % 2 == 0:
-                node_passes(1, w2_q, c, False)
             for t in T_ORDER:
-                h_pass(c, t, w3_q, codes[:], scales[:], False, c % 2 == 0 and t == T_ORDER[-1])
-            if c % 2 == 1:
-                node_passes(1, w2_q, c, True)
+                h_pass(c, t, w3_q, codes[:], scales[:], False, t == T_ORDER[-1])
 
         def edge_half(a):
             grouped = [edge_chunk(2 * a + s) for s in range(2)]

@@ -36,7 +36,7 @@ def tile_picked_edgeup_relu_po_kernel(
         psum = ctx.enter_context(tc.psum_pool(name="psum", bufs=1))
 
         def sb(name, shape, dtype):
-            return keep.tile(shape, dtype, name=name, align_bytes=256)
+            return keep.tile(shape, dtype, name=name, align_bytes=1024)
 
         offsets = keep.tile([P, S // 16], U16, name="offsets")
         node_words = sb("node_words", [P, T], U32)

@@ -20,7 +20,7 @@ CHUNK = 128
 N_CHUNKS = V // CHUNK
 HALF = V // 2
 E_SPLIT = (0, 0, 32, 32)
-Y_SPLIT = 24
+Y_SPLIT = 28
 
 
 def quantize(nc, codes, scales, values):
@@ -232,7 +232,7 @@ def tile_picked_edgeup_relu_po_kernel(
             else:
                 nc.scalar.copy(dst, bank[:, : len(ts), :])
 
-        late_banks = [psum.tile([P, 2, HALF], F32, name="h_bank%d" % u) for u in range(3)]
+        late_banks = [psum.tile([P, 2, HALF], F32, name="h_bank%d" % u) for u in range(2)]
         for t in range(2):
             out_slices(out_banks[2 + t], (t,), 0, False)
             nc.sync.dma_start(out_rows[:, t, :HALF], result[:, t, :HALF])
@@ -240,8 +240,7 @@ def tile_picked_edgeup_relu_po_kernel(
         nc.sync.dma_start(out_rows[:, :2, HALF:], result[:, :2, HALF:])
         out_slices(out_banks[1], (2,), 0, True)
         out_slices(late_banks[0], (3,), 0, True)
-        out_slices(late_banks[1], (2,), 1, False)
-        out_slices(late_banks[2], (3,), 1, True)
+        out_slices(late_banks[1], (2, 3), 1, False)
         nc.sync.dma_start(out_rows[:, 2:, :], result[:, 2:, :])
 
         y_codes = sb("y_codes", [P, V], U32)

@@ -192,8 +192,8 @@ def tile_picked_edgeup_relu_po_kernel(
         def hidden_half(a):
             grouped = sb("h_grouped%d" % a, [P, HALF * PACK], BF16)
             for s in range(2):
-                dst = grouped[:, s * CHUNK * PACK : (s + 1) * CHUNK * PACK].rearrange("p (v t) -> p v t", t=PACK)
-                nc.scalar.activation(dst, h_banks[2 * a + s][:].rearrange("p t v -> p v t"), RELU)
+                dst = grouped[:, s * CHUNK * PACK : (s + 1) * CHUNK * PACK].rearrange("p (g i t) -> p g t i", i=2, t=PACK)
+                nc.scalar.activation(dst, h_banks[2 * a + s][:].rearrange("p t (g i) -> p g t i", i=2), RELU)
             cols = slice(a * HALF, (a + 1) * HALF)
             quantize(nc, h_codes[:, cols], h_scales[:, cols], grouped[:])
 

@@ -235,13 +235,14 @@ def tile_picked_edgeup_relu_po_kernel(
         late_banks = [psum.tile([P, 2, HALF], F32, name="h_bank%d" % u) for u in range(2)]
         for t in range(2):
             out_slices(out_banks[2 + t], (t,), 0, False)
-            nc.sync.dma_start(out_rows[:, t, :HALF], result[:, t, :HALF])
+        nc.sync.dma_start(out_rows[:, :2, :HALF], result[:, :2, :HALF])
         out_slices(out_banks[0], (0, 1), 1, False)
         nc.sync.dma_start(out_rows[:, :2, HALF:], result[:, :2, HALF:])
         out_slices(out_banks[1], (2,), 0, True)
         out_slices(late_banks[0], (3,), 0, True)
+        nc.sync.dma_start(out_rows[:, 2:, :HALF], result[:, 2:, :HALF])
         out_slices(late_banks[1], (2, 3), 1, False)
-        nc.sync.dma_start(out_rows[:, 2:, :], result[:, 2:, :])
+        nc.sync.dma_start(out_rows[:, 2:, HALF:], result[:, 2:, HALF:])
 
         y_codes = sb("y_codes", [P, V], U32)
         y_scales = sb("y_scales", [P, V], U8)

from contextlib import ExitStack

import concourse.mybir as mybir

K, T, S, V, H = 512, 2048, 1024, 512, 512
FLOPS = 4 * 2 * 512 * 512 * 512

F32 = mybir.dt.float32
BF16 = mybir.dt.bfloat16
U32 = mybir.dt.uint32
I32 = mybir.dt.int32
U16 = mybir.dt.uint16
U8 = mybir.dt.uint8
FP8X4 = mybir.dt.float8_e4m3fn_x4
RELU = mybir.ActivationFunctionType.Relu

P = 128
PACK = 4
CHUNK = 128
N_CHUNKS = V // CHUNK
HALF = V // 2
E_SPLIT = (0, 0, 32, 32)
Y_SPLIT = 28


def quantize(nc, codes, scales, values):
    nc.vector.quantize_mx(out=codes.bitcast(FP8X4), scales=scales, in_=values)


def tile_picked_edgeup_relu_po_kernel(
    tc, x_words, x_scales, eT, w1, w2, w3, w4, offs, out_0, out_1, out_2
):
    nc = tc.nc
    with ExitStack() as ctx:
        keep = ctx.enter_context(tc.tile_pool(name="keep", bufs=1))
        psum = ctx.enter_context(tc.psum_pool(name="psum", bufs=1))

        def sb(name, shape, dtype):
            return keep.tile(shape, dtype, name=name, align_bytes=1024)

        offsets = keep.tile([P, S // 16], U16, name="offsets")
        node_words = sb("node_words", [P, T], U32)
        node_scales = sb("node_scales", [P, T], U8)

        nc.vector.memset(node_scales[:].bitcast(I32), 0)

        def load_rows(name, src):
            raw = sb(name, [P, PACK, src.shape[1]], F32)
            nc.sync.dma_start(raw[:], src.rearrange("(p j) c -> p j c", j=PACK))
            return raw[:]

        words_dram = x_words[0].rearrange("p n t -> p (n t)").bitcast(I32)
        nc.sync.dma_start(node_words[:, : T // 2].bitcast(I32), words_dram[:, : T // 2])
        nc.sync.dma_start(offsets[:], offs)
        nc.sync.dma_start(node_scales[0:P:8, :].bitcast(I32), x_scales[0].bitcast(I32))
        nc.sync.dma_start(node_words[:, T // 2 :].bitcast(I32), words_dram[:, T // 2 :])
        w1_raw = load_rows("w1_raw", w1)
        w2_raw = load_rows("w2_raw", w2)
        ON_VECTOR = {0: (96, 0), 1: (P, 0), 2: (44, P)}

        picked_scales = sb("picked_scales", [P, S], U8)
        end_scales = sb("end_scales", [P, S], U8)
        end_words = sb("end_words", [P, S], U32)
        nc.vector.tensor_copy(picked_scales[:], node_scales[:].indirect(offsets[:]))
        nc.vector.tensor_copy(end_scales[:].bitcast(I32), picked_scales[:].bitcast(I32))
        for r in range(1, 4):
            nc.sync.dma_start(
                end_scales[r:P:32, :].bitcast(I32),
                picked_scales[8 * r : P : 32, :].bitcast(I32),
            )
        late = sb("node_scales", [P, 3 * PACK * H], F32)

        def load_late(first, src):
            width = src.shape[1]
            raw = late[:, first : first + PACK * width].rearrange("p (j c) -> p j c", j=PACK)
            nc.sync.dma_start(raw, src.rearrange("(p j) c -> p j c", j=PACK))
            return raw

        w_raw = [[w1_raw], [w2_raw], [load_late(0, w3)]]
        e_raw = [load_late(PACK * (H + a * HALF), eT[:, a * HALF : (a + 1) * HALF]) for a in range(2)]
        w_raw.append([load_late(PACK * (H + V + a * HALF), w4[:, a * HALF : (a + 1) * HALF]) for a in range(2)])

        def quantize_weight(i):
            names = ["w%d_grouped%d" % (i, u) for u in range(2)]
            if i == 1:
                names[0] = "w0_grouped0"
            grouped = [sb(name, [P, 2 * P * PACK], BF16) for name in names]
            m0 = 0
            for n, raw in enumerate(w_raw[i]):
                src = raw.rearrange("p j (m t) -> p m j t", t=PACK)
                m1 = m0 + src.shape[1]
                for u in (1, 0):
                    dst = grouped[u][:].rearrange("p (t m j) -> p m j t", t=2, j=PACK)[:, m0:m1, :, :]
                    pair = src[:, :, :, 2 * u : 2 * u + 2]
                    split = ON_VECTOR[i][u]
                    if split > 0:
                        nc.vector.tensor_copy(dst[:, :split], pair[:, :split])
                    if split < P:
                        nc.scalar.copy(dst[:, split:], pair[:, split:])
                m0 = m1
            parts = {}
            for u in (1, 0):
                codes = sb("w%d_codes%d" % (i, u), [P, 2 * P], U32)
                scales = sb("w%d_scales%d" % (i, u), [P, 2 * P], U8)
                quantize(nc, codes[:], scales[:], grouped[u][:])
                for s in range(2):
                    parts[2 * u + s] = (codes[:, s * P : (s + 1) * P], scales[:, s * P : (s + 1) * P])
            return parts

        h_banks = [psum.tile([P, PACK, CHUNK], F32, name="h_bank%d" % c) for c in range(N_CHUNKS)]
        T_ORDER = (2, 3, 0, 1)

        def h_pass(c, t, weight, codes, scales, start, stop):
            nc.tensor.matmul_mx(
                out=h_banks[c][:, t, :],
                lhsT=weight[t][0].bitcast(FP8X4),
                lhsT_scale=weight[t][1],
                rhs=codes.bitcast(FP8X4),
                rhs_scale=scales,
                start=start,
                stop=stop,
            )

        def node_passes(side, weight):
            for ts in (T_ORDER[:2], T_ORDER[2:]):
                for c in range(N_CHUNKS):
                    cols = slice(side * V + c * CHUNK, side * V + (c + 1) * CHUNK)
                    for t in ts:
                        h_pass(c, t, weight, end_words[:, cols], end_scales[:, cols], side == 0 and t == T_ORDER[0], False)

        out_banks = [psum.tile([P, 2, HALF], F32, name="out_bank%d" % n) for n in range(4)]

        def warm(count, codes, scales, moving, moving_scales):
            for n in range(count):
                nc.tensor.matmul_mx(
                    out=out_banks[n][:].rearrange("p s v -> p (s v)")[:, : moving.shape[1]],
                    lhsT=codes.bitcast(FP8X4),
                    lhsT_scale=scales,
                    rhs=moving.bitcast(FP8X4),
                    rhs_scale=moving_scales,
                    start=True,
                    stop=True,
                )

        nc.vector.tensor_copy(end_words[:], node_words[:].indirect(offsets[:]))
        w1_q = quantize_weight(0)
        node_passes(0, w1_q)
        node_passes(1, quantize_weight(1))
        w3_q = quantize_weight(2)

        h_codes = sb("h_codes", [P, V], U32)
        h_scales = sb("h_scales", [P, V], U8)

        def edge_chunk(c):
            a, s = divmod(c, 2)
            grouped = sb("e_grouped%d" % c, [P, CHUNK * PACK], BF16)
            src = e_raw[a][:, :, s * CHUNK : (s + 1) * CHUNK].rearrange("p j (g i) -> p g j i", i=4)
            dst = grouped[:].rearrange("p (g i j) -> p g j i", i=4, j=PACK)
            if E_SPLIT[c] > 0:
                nc.vector.tensor_copy(dst[:, : E_SPLIT[c]], src[:, : E_SPLIT[c]])
            if E_SPLIT[c] < CHUNK // 4:
                nc.scalar.copy(dst[:, E_SPLIT[c] :], src[:, E_SPLIT[c] :])
            return grouped

        def edge_passes(c, grouped):
            codes = sb("e_codes%d" % c, [P, CHUNK], U32)
            scales = sb("e_scales%d" % c, [P, CHUNK], U8)
            quantize(nc, codes[:], scales[:], grouped[:])
            for t in T_ORDER:
                h_pass(c, t, w3_q, codes[:], scales[:], False, t == T_ORDER[-1])

        def edge_half(a):
            grouped = [edge_chunk(2 * a + s) for s in range(2)]
            for s in range(2):
                edge_passes(2 * a + s, grouped[s])

        w4_codes = [sb("w4_codes%d" % t, [P, P], U32) for t in range(PACK)]
        w4_scales = [sb("w4_scales%d" % t, [P, P], U8) for t in range(PACK)]

        w4_grouped = [sb("w4_grouped%d" % u, [P, 2, H], BF16) for u in range(2)]

        def round_w4(n):
            src = w_raw[3][n].rearrange("p j (m t) -> p m j t", t=PACK)
            for u in range(2):
                dst = w4_grouped[u][:].rearrange("p t (m j) -> p m j t", j=PACK)[:, n * P // 2 : (n + 1) * P // 2]
                nc.vector.tensor_copy(dst, src[:, :, :, 2 * u : 2 * u + 2])

        def quantize_w4(t, first, last):
            values = w4_grouped[t // 2][:, t % 2, first * PACK : last * PACK]
            quantize(nc, w4_codes[t][:, first:last], w4_scales[t][:, first:last], values)

        def hidden_half(a):
            grouped = sb("h_grouped%d" % a, [P, HALF * PACK], BF16)
            for s in range(2):
                dst = grouped[:, s * CHUNK * PACK : (s + 1) * CHUNK * PACK].rearrange("p (g i t) -> p g t i", i=2, t=PACK)
                nc.scalar.activation(dst, h_banks[2 * a + s][:].rearrange("p t (g i) -> p g t i", i=2), RELU)
            cols = slice(a * HALF, (a + 1) * HALF)
            quantize(nc, h_codes[:, cols], h_scales[:, cols], grouped[:])

        for a in range(2):
            edge_half(a)
        round_w4(0)
        for t in range(2):
            quantize_w4(t, 0, P // 2)
        hidden_half(0)
        warm(3, h_codes[:, :P], h_scales[:, :P], h_codes[:, :HALF], h_scales[:, :HALF])
        round_w4(1)
        for t in range(2):
            quantize_w4(t, P // 2, P)
        hidden_half(1)
        for t in (2, 3):
            quantize_w4(t, 0, P)

        out_rows = out_0.rearrange("(p t) v -> p t v", t=PACK)
        result = sb("result", [P, PACK, V], F32)

        def out_slices(bank, ts, a, on_vector):
            cols = slice(a * HALF, (a + 1) * HALF)
            for s, t in enumerate(ts):
                nc.tensor.matmul_mx(
                    out=bank[:, s, :],
                    lhsT=w4_codes[t][:].bitcast(FP8X4),
                    lhsT_scale=w4_scales[t][:],
                    rhs=h_codes[:, cols].bitcast(FP8X4),
                    rhs_scale=h_scales[:, cols],
                    start=True,
                    stop=True,
                )
            dst = result[:, ts[0] : ts[-1] + 1, cols]
            if on_vector:
                nc.vector.tensor_copy(dst, bank[:, : len(ts), :])
            else:
                nc.scalar.copy(dst, bank[:, : len(ts), :])

        late_banks = [psum.tile([P, 2, HALF], F32, name="h_bank%d" % u) for u in range(2)]
        for t in range(2):
            out_slices(out_banks[2 + t], (t,), 0, False)
        nc.sync.dma_start(out_rows[:, :2, :HALF], result[:, :2, :HALF])
        out_slices(out_banks[0], (0, 1), 1, False)
        nc.sync.dma_start(out_rows[:, :2, HALF:], result[:, :2, HALF:])
        out_slices(out_banks[1], (2,), 0, True)
        out_slices(late_banks[0], (3,), 0, True)
        nc.sync.dma_start(out_rows[:, 2:, :HALF], result[:, 2:, :HALF])
        out_slices(late_banks[1], (2, 3), 1, False)
        nc.sync.dma_start(out_rows[:, 2:, HALF:], result[:, 2:, HALF:])

        y_codes = sb("y_codes", [P, V], U32)
        y_scales = sb("y_scales", [P, V], U8)
        codes_dram = out_1[0].rearrange("p n t -> p (n t)").bitcast(I32)
        y_grouped = [sb("y_grouped%d" % a, [P, HALF * PACK], BF16) for a in range(2)]

        def y_views(a):
            src = result[:, :, a * HALF : (a + 1) * HALF].rearrange("p t (g i) -> p g t i", i=4)
            dst = y_grouped[a][:].rearrange("p (g i t) -> p g t i", i=4, t=PACK)
            return dst, src

        dst, src = y_views(0)
        nc.vector.tensor_copy(dst, src)
        dst, src = y_views(1)
        nc.vector.tensor_copy(dst[:, :Y_SPLIT], src[:, :Y_SPLIT])
        nc.scalar.copy(dst[:, Y_SPLIT:], src[:, Y_SPLIT:])
        for a in range(2):
            cols = slice(a * HALF, (a + 1) * HALF)
            quantize(nc, y_codes[:, cols], y_scales[:, cols], y_grouped[a][:])
            nc.sync.dma_start(codes_dram[:, cols], y_codes[:, cols].bitcast(I32))
        for q in range(4):
            queue = nc.sync if q % 2 == 0 else nc.scalar
            queue.dma_start(
                out_2[0][4 * q : 4 * q + 4, :].bitcast(I32),
                y_scales[32 * q : 32 * q + 4, :].bitcast(I32),
            )
